import numpy as np, ml_dtypes
CORES = [1,5,17,21,33,37,49,53]
N = 8
BF = ml_dtypes.bfloat16
W, L, CAP, T, D = 8192, 192, 3, 4, 3
def place(s, p):
    return ((((s & 4095) * (2 * p + 1)) >> 3) + 37 * s + 613 * p) & (W - 1)
def cells(lf, p):
    return place((32768 + lf)[..., None] >> np.arange(16), p[..., None])
def page(w, z):
    return np.add.reduce(w[..., 0:1] * z, axis=-2) & 255
def pack(x, c, z, lf, w, th):
    return {"x0": x.reshape(N, 128, W).astype(np.float32).astype(BF), "c0": c.reshape(N, 8, W).astype(np.float32).astype(BF), "z0": z.reshape(N, 128, L).astype(np.float32).astype(BF),
            "leaf": np.ascontiguousarray(lf).astype(np.int32), "wt": np.ascontiguousarray(w.reshape(N, 128, 2)).astype(np.int32), "th": np.ascontiguousarray(th.reshape(N, 8, 1)).astype(np.int32)}
def parts(rng):
    x = rng.integers(0, 16, (N, 8, 16, W)); c = rng.integers(0, CAP, (N, 8, W))
    pool = rng.integers(0, 16, (N, 8, 16, 64)); z = np.take_along_axis(pool, rng.integers(0, 64, (N, 8, 1, L)), 3)
    z = np.where(rng.random((N, 8, 1, L)) < 0.5, z, rng.integers(0, 16, (N, 8, 16, L)))
    few = rng.integers(0, 32768, (N, 8, 16)); lf = np.take_along_axis(few, rng.integers(0, 16, (N, 8, L)), 2)
    lf = np.where(rng.random((N, 8, L)) < 0.25, lf, rng.integers(0, 32768, (N, 8, L)))
    return x, c, z, lf, rng.integers(1, 256, (N, 8, 16, 2)), rng.integers(50, 81, (N, 8))
def setup_inputs(rng):
    return pack(*parts(rng))
def setup_inputs_spread(rng):
    def uneven(n):
        v = np.minimum((np.exp2(4 * rng.random((N, 8, 1, n))) * rng.random((N, 8, 16, n))).astype(np.int64), 15)
        return np.where(rng.random((N, 8, 1, n)) < 0.5, v, 15 - v)
    c = np.where(rng.random((N, 8, W)) < rng.random((N, 8, 1)), CAP - 1, rng.integers(0, CAP, (N, 8, W)))
    lf = np.minimum(np.exp2(15 * rng.random((N, 8, L))).astype(np.int64), 32767)
    w = np.minimum(np.maximum(np.exp2(8 * rng.random((N, 8, 16, 2))).astype(np.int64), 1), 255)
    return pack(uneven(W), c, uneven(L), lf, w, rng.integers(0, 121, (N, 8)))
def setup_inputs_ends(rng):
    def ends(n):
        one = rng.integers(0, 2, (N, 8, 1, n)); el = rng.integers(0, 2, (N, 8, 16, n))
        return np.where(rng.random((N, 8, 1, n)) < 0.5, one, el) * 15
    x = ends(W); z = ends(L); c = (CAP - 1) * rng.integers(0, 2, (N, 8, W)); lf = 32767 * rng.integers(0, 2, (N, 8, L))
    w = 1 + 254 * rng.integers(0, 2, (N, 8, 16, 2)); w[:, 1::3] = 255; w[:, 0, 0] = 1; w[:, 0, 15] = 255
    th = 120 * ((np.arange(8)[None, :] + rng.integers(0, 2, (N, 1))) & 1)
    for q in range(N):
        for g in range(8):
            if g % 3 == 1:
                z[q, g][:, [1, L - 2]] = 15; lf[q, g, [1, L - 2]] = 32767
                x[q, g][:, cells(np.array([32767]), np.array([(16 * 15 * 255) & 255]))[0]] = 0
            z[q, g][:, [2, L - 3]] = 0; lf[q, g, [2, L - 3]] = 0
            order = rng.permutation(16)
            for m in (16, 0) + tuple(range(1, 16)):
                v = 15 * (order < m).astype(np.int64); p = int(np.dot(w[q, g, :, 0], v)) & 255
                k = np.flatnonzero(place(32768 + np.arange(32768), p) == W - 1)
                if k.size:
                    lone = int(rng.choice(k))
                    z[q, g][:, [0, L - 1]] = v[:, None]; lf[q, g, [0, L - 1]] = lone
                    x[q, g][:, W - 1] = v if (q + g) % 2 == 0 else 15 - v
                    above = int(place((32768 + lone) >> 1, p))
                    if (q + g) % 2 == 1 and above != W - 1:
                        x[q, g][:, above] = v; c[q, g, W - 1] = CAP - 1
                    break
    return pack(x, c, z, lf, w, th)
def near(z, n):
    i = np.arange(16)[:, None]; d = (n >> 4)[None, :] + (i < (n & 15)[None, :])
    return np.where(z < 8, z + d, z - d)
def setup_inputs_corners(rng):
    x, c, z, lf, w, th = parts(rng)
    th = rng.choice(np.array([0, 1, 20, 40, 120]), (N, 8)); kind = (np.arange(8)[None, :] + rng.integers(0, 3, (N, 1))) % 3
    c = np.where(kind[:, :, None] == 0, 0, np.where(kind[:, :, None] == 1, CAP - 1, c))
    lf = np.where(rng.random((N, 8, L)) < 0.5, rng.choice(np.array([0, 1, 16383, 16384, 32766, 32767]), (N, 8, L)), lf); lf[:, :, 0] = 0; lf[:, :, L - 1] = 32767
    wk = rng.integers(0, 4, (N, 8, 1, 2)); w = np.where(wk == 0, 1, np.where(wk == 1, 255, w))
    zk = rng.random((N, 8, 1, L)); z = np.where(zk < 0.05, 0, np.where(zk > 0.95, 15, z))
    for q in range(N):
        for g in range(8):
            h = cells(lf[q, g], page(w[q, g], z[q, g]))
            lv = rng.choice(np.array([0, 1, 7, 14]), L); n = np.maximum(th[q, g] + rng.integers(-1, 2, L), 0)
            x[q, g][:, h[np.arange(L), lv]] = near(z[q, g], n)
            e = np.array([th[q, g], th[q, g] + 1])
            x[q, g][:, h[[0, L - 1], 0]] = near(z[q, g][:, [0, L - 1]], e)
    return pack(x, c, z, lf, w, th)
def setup_inputs_crowd(rng):
    x, c, z, lf, w, th = parts(rng)
    for q in range(N):
        if q % 3 < 2:
            x[q] = rng.integers(0, 4, (8, 16, W)); z[q] = rng.integers(12, 16, (8, 16, L)); th[q] = rng.integers(0, 61, 8)
        lone = 0 if q & 1 else L - 1
        for g in range(8):
            if g % 4 == 0: ix = np.full(L, int(rng.integers(0, L)))
            elif g % 4 == 1: ix = np.full(L, lone ^ 1); ix[lone] = lone
            elif g % 4 == 2: ix = rng.integers(0, 4, L)
            else: ix = np.arange(L)
            z[q, g] = z[q, g][:, ix]; lf[q, g] = lf[q, g][ix]
            if q % 3 == 1 and g == 1:
                pg = page(w[q, g], z[q, g]); other = cells(lf[q, g, [lone ^ 1]], pg[[lone ^ 1]])[0]
                some = rng.permutation(32768)[:256]; hs = place(32768 + some, pg[lone])
                k = int(np.argmax(~np.isin(hs, other)))
                lf[q, g, lone] = some[k]; x[q, g][:, hs[k]] = z[q, g][:, lone]
    return pack(x, c, z, lf, w, th)
def setup_inputs_full(rng):
    x, c, z, lf, w, th = parts(rng); th = rng.integers(0, 9, (N, 8)); c[:, [0, 1, 4, 5]] = CAP - 1
    for q in range(N):
        for g in range(8):
            a, b = rng.permutation(16)[:2]; w[q, g, a, 0] = 1; w[q, g, b, 0] = 16
            zz = rng.integers(0, 16, (16, L)); zz[[a, b]] = 0
            pg = np.full(L, int(rng.integers(0, 256))) if g % 4 == 3 else rng.permutation(256)[:L]
            left = (pg - page(w[q, g], zz)) & 255; zz[a] = left & 15; zz[b] = left >> 4; z[q, g] = zz
            cand = rng.integers(0, 32768, (L, 24)); lv = rng.integers(1, 16, (L, 24))
            if g % 2 == 0: lv[:, :16] = 15
            h = cells(cand, pg[:, None]).tolist(); lv = lv.tolist(); taken = set(); hits = set(); at = []; who = []
            for l in range(L):
                for m in range(24):
                    v = lv[l][m]; way = h[l][m]
                    if way[v - 1] not in taken and (v == 15 or (way[v] not in hits and way[v] not in way[:v])): break
                lf[q, g, l] = cand[l, m]; taken.add(way[v - 1])
                if v < 15: hits.add(way[v]); at.append(way[v]); who.append(l)
            if at: x[q, g][:, np.array(at)] = near(zz[:, np.array(who)], rng.integers(0, int(th[q, g]) + 1, len(at)))
    return pack(x, c, z, lf, w, th)
def check_inputs(d):
    bad = []
    for k, lo, hi in (("x0", 0, 15), ("c0", 0, CAP - 1), ("z0", 0, 15), ("leaf", 0, 32767), ("wt", 1, 255), ("th", 0, 120)):
        a = np.asarray(d[k]).astype(np.float64)
        if not (np.min(a) >= lo and np.max(a) <= hi): bad.append("range of " + k)
        elif np.any(a != np.floor(a)): bad.append("whole numbers in " + k)
    return bad
def reference(x0, c0, z0, leaf, wt, th):
    X = x0.astype(np.float32).astype(np.int64).reshape(N, 8, 16, W); C = c0.astype(np.float32).astype(np.int64).reshape(N, 8, W)
    z = z0.astype(np.float32).astype(np.int64).reshape(N, 8, 16, L); lf = leaf.astype(np.int64)
    w = wt.astype(np.int64).reshape(N, 8, 16, 2); lim = th.astype(np.int64).reshape(N, 8, 1, 1); A = np.zeros(N, np.int64); zs = []
    for t in range(T):
        home = (np.arange(N) - D * t) % N
        zq = z[home]; lq = lf[home]
        h = cells(lq, page(w, zq))
        xk = np.take_along_axis(X, h.reshape(N, 8, 1, L * 16), 3).reshape(N, 8, 16, L, 16)
        dist = np.add.reduce(np.abs(xk - zq[..., None]), axis=2)
        hit = dist <= lim + (A & 15).reshape(N, 1, 1, 1); hit[..., 15] = True
        j = np.argmax(hit, axis=-1)
        y = np.take_along_axis(xk, j[:, :, None, :, None], 4)[..., 0]
        for q in range(N):
            for g in range(8):
                m = np.flatnonzero(j[q, g] > 0); named = h[q, g, m, j[q, g, m] - 1]
                cell, first = np.unique(named, return_index=True); who = m[first]
                C[q, g, cell] += 1; full = C[q, g, cell] == CAP
                X[q, g][:, cell[full]] = y[q, g][:, who[full]]; C[q, g, cell[full]] = 0
                cell, first = np.unique(h[q, g, :, 15], return_index=True)
                X[q, g][:, cell] = (xk[q, g][:, first, 15] + zq[q, g][:, first]) >> 1
        A = np.add.reduce((j == 15).astype(np.int64).reshape(N, 8 * L), axis=1)
        zq = np.abs(zq - y); z = np.zeros_like(zq); z[home] = zq; zs.append(z)
        if t < T - 1: lf[home] = (8 * lq + np.add.reduce(w[..., 1:2] * zq, axis=2)) & 32767
    return {"zs": np.concatenate(zs, axis=3).reshape(N, 128, T * L).astype(np.float32).astype(BF), "xs": np.add.reduce(w[..., 0:1] * X, axis=2).astype(np.float32), "cs": C.astype(np.float32)}

from concourse.mybir import AluOpType, ActivationFunctionType, AxisListType

A = AluOpType
F = ActivationFunctionType
N, W, L, STEPS, HOP = 8, 8192, 192, 4, 3
WD = W + 256
BIG = 16384.0
NC = L // 16
SEG = [160 * (c // 4) + 8 * (c % 4) * (c % 4 + 1) for c in range(NC)]
OWN = 12
LATE = 1
DZS = False
PIECES = 4

SCRATCH = {
    "X": ("sbuf", [128, WD], "bfloat16"), "C": ("sbuf", [128, WD], "bfloat16"),
    "raw": ("sbuf", [128, 16 * L], "bfloat16"), "mx": ("sbuf", [128, 15 * L], "bfloat16"),
    "wti": ("sbuf", [128, 4], "int32"), "wprev": ("sbuf", [128, 4], "int32"),
    "wf": ("sbuf", [128, 4], "float32"), "bf": ("sbuf", [128, 4], "float32"),
    "lfi": ("sbuf", [8, L], "int32"), "lff": ("sbuf", [8, L], "float32"),
    "thi": ("sbuf", [8, 4], "int32"), "thf": ("sbuf", [8, 4], "float32"),
    "colf": ("sbuf", [128, L], "float32"), "c16": ("sbuf", [128, L], "float32"), "c12": ("sbuf", [128, L], "float32"),
    "blk": ("sbuf", [128, 128], "float32"), "pi": ("sbuf", [128, 16], "int32"), "pj": ("sbuf", [128, 16], "int32"),
    "col": ("sbuf", [128, 32], "float32"), "base": ("sbuf", [128, 144], "float32"),
    "b2": ("sbuf", [128, 144], "bfloat16"), "bn": ("sbuf", [128, 144], "bfloat16"), "ba": ("sbuf", [128, 144], "bfloat16"),
    "bb": ("sbuf", [128, 144], "bfloat16"), "bfull": ("sbuf", [128, 144], "bfloat16"),
    "b8": ("sbuf", [8, 144], "float32"), "o8": ("sbuf", [8, 128], "float32"),
    "onesn": ("sbuf", [128, 128], "bfloat16"), "onesf": ("sbuf", [128, 128], "float32"),
    "row": ("sbuf", [128, 16 * 128], "bfloat16"), "half0": ("sbuf", [128, 160], "bfloat16"), "half1": ("sbuf", [128, 160], "bfloat16"),
    "diagf": ("sbuf", [128, 16], "float32"), "colb": ("sbuf", [128, 16], "bfloat16"), "pfb": ("sbuf", [128, 16], "bfloat16"),
    "wnew": ("sbuf", [128, 128], "bfloat16"), "ident": ("sbuf", [128, 128], "bfloat16"),
    "identn": ("sbuf", [128, 128], "bfloat16"), "all": ("sbuf", [128, 128], "float32"), "tmp": ("sbuf", [128, L], "float32"), "tmp2": ("sbuf", [128, L], "float32"),
    "diag": ("sbuf", [128, L], "bfloat16"),
    "pw": ("sbuf", [128, L], "float32"), "keep": ("sbuf", [128, L], "float32"),
    "two": ("sbuf", [128, 480], "bfloat16"), "one": ("sbuf", [128, 480], "bfloat16"), "spare": ("sbuf", [128, 32], "float32"),
    "js": ("sbuf", [128, L], "bfloat16"), "top": ("sbuf", [128, 16], "bfloat16"),
    "bigb": ("sbuf", [128, 16], "bfloat16"), "own": ("sbuf", [128, 16], "float32"),
    "rep": ("sbuf", [128, 16], "uint16"), "rep2": ("sbuf", [128, 16], "uint16"), "back": ("sbuf", [128, 16], "uint16"),
    "ends": ("sbuf", [128, 2], "uint16"),
    "s1": ("sbuf", [128, 16], "float32"), "s2": ("sbuf", [128, 16], "float32"), "s3": ("sbuf", [128, 16], "float32"),
    "s4": ("sbuf", [128, 16], "float32"), "si": ("sbuf", [128, 16], "int32"), "sj": ("sbuf", [128, 16], "int32"),
    "gp": ("sbuf", [128, 16], "int32"), "jp": ("sbuf", [128, 16], "int32"),
    "gf": ("sbuf", [128, 16], "int32"), "jf": ("sbuf", [128, 16], "int32"),
    "qw": ("sbuf", [128, 16], "float32"), "rw": ("sbuf", [128, 64], "float32"), "pf": ("sbuf", [128, 16], "float32"),
    "sp": ("sbuf", [128, L], "int32"), "s12": ("sbuf", [128, L], "int32"), "bit": ("sbuf", [128, 48], "int32"),
    "w1": ("sbuf", [128, L], "float32"), "w2": ("sbuf", [128, L], "int32"),
    "hw": ("sbuf", [128, 208], "int32"), "hu": ("sbuf", [128, L], "uint16"),
    "gm": ("sbuf", [128, L], "float32"), "ks": ("sbuf", [128, L], "float32"),
    "turned": ("sbuf", [128, L], "bfloat16"), "miss": ("sbuf", [128, L], "bfloat16"), "acc": ("sbuf", [128, 4], "float32"),
    "mi": ("sbuf", [128, 4], "int32"), "mj": ("sbuf", [128, 4], "int32"), "mcol": ("sbuf", [128, 4], "float32"),
    "thc": ("sbuf", [128, 4], "float32"),
    "offu": ("sbuf", [128, 16], "uint16"), "off2": ("sbuf", [128, 16], "uint16"), "keyu": ("sbuf", [128, 16], "uint16"),
    "dz": ("sbuf", [128, L], "bfloat16"), "yv": ("sbuf", [128, L], "bfloat16"), "cr": ("sbuf", [128, L], "bfloat16"),
    "nc": ("sbuf", [128, L], "bfloat16"), "r1": ("sbuf", [128, L], "bfloat16"), "rv": ("sbuf", [128, L], "bfloat16"),
    "en": ("sbuf", [128, 480], "bfloat16"), "er": ("sbuf", [128, 480], "bfloat16"),
    "sn": ("sbuf", [128, 480], "bfloat16"), "sr": ("sbuf", [128, 480], "bfloat16"),
    "ln": ("sbuf", [128, 16], "float32"), "lr": ("sbuf", [128, 16], "float32"),
    "an": ("sbuf", [128, 32], "float32"), "an2": ("sbuf", [128, 32], "float32"), "nu": ("sbuf", [128, 32], "uint16"),
    "ar": ("sbuf", [128, 16], "float32"), "ar2": ("sbuf", [128, 16], "float32"), "ru": ("sbuf", [128, 16], "uint16"),
}
for _t in range(STEPS):
    SCRATCH["zin%d" % _t] = ("sbuf", [128, L], "bfloat16")
    SCRATCH["zout%d" % _t] = ("sbuf", [128, L], "bfloat16")
    SCRATCH["fout%d" % _t] = ("sbuf", [128, NC], "float32")
SCRATCH["fin"] = ("sbuf", [128, STEPS * NC], "float32")
SCRATCH["home"] = ("sbuf", [128, STEPS * L], "bfloat16")
SCRATCH["xo"] = ("sbuf", [128, 512], "float32")
for _b in ("pz", "pd", "pt", "po", "pp", "pk", "pr", "pn"):
    SCRATCH[_b] = ("psum", [128, 512], "float32")

SEMAPHORES = ["v", "s", "p", "g", "lx", "lz", "lw", "ll", "lt", "lc", "aw", "ow", "oc"]
SEMAPHORES += ["ox%d" % _t for _t in range(PIECES)]
for _t in range(STEPS):
    SEMAPHORES += ["az%d" % _t, "af%d" % _t, "ah%d" % _t, "oz%d" % _t, "of%d" % _t, "oh%d" % _t, "st%d" % _t]


def rank_program(g, core, T, topo):
    rank = T.rank_of(core)
    if rank is None:
        return
    Q = {"v": g.vector, "s": g.scalar, "p": g.tensor, "g": g, "y": g.sync}
    count = {"v": 0, "s": 0, "p": 0, "g": 0}
    known = {q: {} for q in Q}
    snap = {}
    wrote, read, bank = {}, {}, {}
    total = {}

    def wait(q, ev):
        if known[q].get(ev[0], 0) >= ev[1]:
            return
        Q[q].wait_ge(T.sem[ev[0]], ev[1])
        for k, v in snap.get(ev, {}).items():
            known[q][k] = max(known[q].get(k, 0), v)
        known[q][ev[0]] = ev[1]

    def order(q, r, w, ps):
        evs = [wrote.get(x) for x in r]
        for x in w:
            evs.append(wrote.get(x))
            evs.extend(read.get(x, []))
        for x in ps:
            evs.extend(ev for e, ev in bank.get(x, {}).items() if e != q)
        for ev in sorted(set(e for e in evs if e is not None), key=lambda e: (-e[1], e[0])):
            wait(q, ev)

    def note(q, ev, r, w, ps):
        snap[ev] = dict(known[q])
        total[ev[0]] = max(total.get(ev[0], 0), ev[1])
        for x in r:
            read.setdefault(x, []).append(ev)
        for x in w:
            wrote[x] = ev
            read[x] = []
        for x in ps:
            bank.setdefault(x, {})[q] = ev

    def op(q, call, r=(), w=(), ps=()):
        order(q, r, w, ps)
        count[q] += 1
        call().then_inc(T.sem[q], 1)
        note(q, (q, count[q]), r, w, ps)

    def dma(q, sem, out, in_, r=(), w=(), **kw):
        order(q, r, w, ())
        Q[q].dma_start(out, in_, **kw).then_inc(T.sem[sem], 16)
        note(q, (sem, total.get(sem, 0) + 16), r, w, ())

    def lanes(a, b):
        return topo.engines(T.cores[a % N], T.cores[b % N])[:8]

    def send(to, out, in_, arrive, leave, r):
        order("g", r, (), ())
        rid, pid, _ = topo.addr(T.cores[to % N])
        eng = lanes(rank, to)
        g.remote_dma(out, in_, T.sem[arrive], T.sem[leave], pid, rid, sum(1 << e for e in eng))
        note("g", (leave, len(eng)), r, (), ())

    def lands(frm, name, arrive):
        wrote[name] = (arrive, len(lanes(frm, rank)))
        total[arrive] = wrote[name][1]

    V, S, P = g.vector, g.scalar, g.tensor

    def ts(out, in0, s1, s2, o0, o1, r, w, ps=()):
        if o1 is None:
            op("v", lambda: V.tensor_scalar(out, in0, s1, None, o0), r, w, ps)
        else:
            op("v", lambda: V.tensor_scalar(out, in0, s1, s2, o0, o1), r, w, ps)

    def tt(out, in0, in1, o, r, w, ps=()):
        op("v", lambda: V.tensor_tensor(out, in0, in1, o), r, w, ps)

    def cp(out, in_, r, w, ps=()):
        op("v", lambda: V.tensor_copy(out, in_), r, w, ps)

    def fill(out, val, w):
        op("v", lambda: V.memset(out, val), (), w)

    def scan(out, d0, d1, init, o0, o1, r, w, ps=()):
        op("v", lambda: V.tensor_tensor_scan(out, d0, d1, init, o0, o1), r, w, ps)

    def mm(out, lhsT, rhs, start, stop, r, b):
        op("p", lambda: P.matmul(out, lhsT, rhs, start, stop), r, (), (b,))

    def act(out, in_, func, r, w, ps=(), **kw):
        op("s", lambda: S.activation(out, in_, func, **kw), r, w, ps)

    def iota(out, pat, base, cm, w, small=True):
        if small:
            op("g", lambda: g.iota(out, pat, base, cm, allow_small_or_imprecise_dtypes=True), (), w)
        else:
            op("g", lambda: g.iota(out, pat, base, cm), (), w)

    def packed(out, base, bname, src, sname, first, b):
        for m in range(16):
            mm(out, base[:, 15 - m:143 - m], src[:, m:L:16], first and m == 0, m == 15, (bname, sname), b)

    def weave(a, b):
        for n in range(max(len(a), len(b))):
            if n < len(a):
                a[n]()
            if n < len(b):
                b[n]()

    nxt, prv = rank + HOP, rank - HOP
    lands(prv, "wprev", "aw")
    for t in range(1, STEPS):
        lands(prv, "zin%d" % t, "az%d" % t)
        lands(prv, "fin%d" % t, "af%d" % t)
        lands(rank + HOP * t, "home%d" % t, "ah%d" % t)

    E = WD // 8
    dma("s", "lw", T.wti[:, 0:2], T.wt[:], (), ("wti",))
    dma("y", "lz", T.zin0[:], T.z0[:], (), ("zin0",))
    dma("s", "ll", T.lfi[:], T.leaf[:], (), ("lfi",))
    dma("y", "lx", T.X[:, 0:W], T.x0[:], (), ("X",))
    iota(T.pi[:, 0:1], [[0, 1]], 0, 1, ("pi",), False)
    iota(T.colf[:], [[1, L]], 0, 0, ("colf",))
    iota(T.c12[:], [[0, 16], [1, NC]], 0, 0, ("c12",))
    iota(T.c16[:], [[0, NC], [1, 16]], 0, 0, ("c16",))
    iota(T.blk[:], [[16, 8], [0, 16]], 0, 0, ("blk",))
    dma("g", "lt", T.thi[:, 0:1], T.th[:], (), ("thi",), allow_slow_non_contiguous=True)
    fill(T.C[:, 0:E], 0.0, ("Ca",))
    fill(T.C[:, E:3 * E], 0.0, ("Cb",))
    act(T.C[:, 3 * E:4 * E], T.C[:, 0:E], F.Copy, ("Ca",), ("Cc",))
    act(T.C[:, 4 * E:6 * E], T.C[:, E:3 * E], F.Copy, ("Cb",), ("Ce",))
    act(T.one[:], T.C[:, 0:480], F.Identity, ("Ca",), ("one",), bias=1.0)
    act(T.two[:], T.C[:, 0:480], F.Identity, ("Ca",), ("two",), bias=2.0)
    act(T.bigb[:], T.C[:, 0:16], F.Identity, ("Ca",), ("bigb",), bias=BIG)
    send(nxt, T.wprev[:, 0:2], T.wti[:, 0:2], "aw", "ow", ("wti",))
    iota(T.C[:, 6 * E:WD], [[0, 2 * E]], 0, 0, ("Cd",))

    CP, CM, CG, CG15, CNM, CCB, CWN, CJ, CFU, CH0, CTHR, CP16, CP15, CH1, CPP = range(15)

    def c(i):
        return T.col[:, i:i + 1]
    cp(c(CP), T.pi[:, 0:1], ("pi",), ("cP",))
    ts(T.pj[:, 0:1], T.pi[:, 0:1], 15, None, A.bitwise_and, None, ("pi",), ("pj0",))
    ts(c(CP15), c(CP), 16.0, 15.0, A.mult, A.add, ("cP",), ("cP15",))
    cp(c(CM), T.pj[:, 0:1], ("pj0",), ("cM",))
    ts(T.b8[:], T.colf[0:8, 0:144], T.col[0:8, CP15:CP15 + 1], None, A.is_equal, None, ("colf", "cP15"), ("b8",))
    tt(c(CG), c(CP), c(CM), A.subtract, ("cP", "cM"), ("cG",))
    cp(T.lff[:], T.lfi[:], ("lfi",), ("lff",))
    ts(c(CG15), c(CG), 15.0, None, A.add, None, ("cG",), ("cG15",))
    cp(T.wf[:, 0:2], T.wti[:, 0:2], ("wti",), ("wf",))
    ts(T.base[:], T.colf[:, 0:144], c(CG15), None, A.is_equal, None, ("colf", "cG15"), ("base",))
    ts(T.wf[:, 2:3], T.wf[:, 0:1], 128.0, None, A.mult, None, ("wf",), ("wa",))
    ts(T.diagf[:], T.colf[:, 0:16], c(CM), None, A.is_equal, None, ("colf", "cM"), ("diagf",))
    ts(T.ba[:], T.base[:], T.wf[:, 2:3], None, A.mult, None, ("base", "wa"), ("ba",))
    ts(T.s1[:], T.colf[:, 0:16], 16.0, c(CM), A.mult, A.add, ("colf", "cM"), ("s1",))
    ts(T.back[:, 0:1], c(CM), -1.0, NC - 1.0, A.mult, A.add, ("cM",), ("back",))
    ts(T.s2[:], T.s1[:], 1.0 / 12, 0.5 / 12 - 0.5, A.mult, A.add, ("s1",), ("s2",))
    ts(T.tmp[:], T.c12[:], 0.0, 0.5, A.is_gt, A.max, ("c12",), ("tmp",))
    cp(T.si[:], T.s2[:], ("s2",), ("si",))
    fill(T.tmp2[:], 0.0, ("tmp2",))
    ts(T.s2[:], T.si[:], -12.0, None, A.mult, None, ("si",), ("s2",))
    scan(T.pw[:], T.tmp[:], T.tmp2[:], 8192.0, A.mult, A.add, ("tmp", "tmp2"), ("pw",))
    tt(T.s3[:], T.s1[:], T.s2[:], A.add, ("s1", "s2"), ("s3",))
    cp(T.rep[:], T.s3[:], ("s3",), ("rep",))
    cp(T.rep2[:, 3:16], T.s3[:, 3:16], ("s3",), ("rep2a",))
    ts(T.rep2[:, 0:3], T.s1[:, 0:3], 16.0, None, A.add, None, ("s1",), ("rep2b",))
    fill(T.rw[:, NC:16], 0.0, ("rwp",))
    ts(T.onesf[:], T.blk[:], c(CG), None, A.is_equal, None, ("blk", "cG"), ("onesf",))
    act(T.onesn[:], T.onesf[:], F.Copy, ("onesf",), ("onesn",), scale=-1.0)
    act(T.b2[:], T.base[:], F.Copy, ("base",), ("b2",), scale=2.0)
    act(T.bn[:], T.base[:], F.Copy, ("base",), ("bn",), scale=-1.0)
    for m in range(16):
        act(T.row[:, 128 * m:128 * m + 128], T.onesf[:], F.Copy, ("onesf", "diagf"), ("row%d" % m,), scale=T.diagf[:, m:m + 1])

    def index(t, rest=()):
        z, fn = "zin%d" % t, "fout%d" % t
        fo = T[fn]
        if t == 0:
            packed(T.pn[:, 0:NC], T.b8, "b8", T.lff, "lff", True, "pn")
        else:
            packed(T.pn[:, 0:NC], T.bb, "bb", T[z], z, True, "pn")
        packed(T.pp[:, 0:NC], T.ba, "ba", T[z], z, True, "pp")
        if t:
            tt(T.gf[:, 0:NC], T.pn[:, 0:NC], T.fin[:, t * NC:(t + 1) * NC], A.add, ("fin%d" % t,), ("gf",), ("pn",))
        else:
            cp(T.gf[:, 0:NC], T.pn[:, 0:NC], (), ("gf",), ("pn",))
        weave(rest[0:1], [])
        ts(T.jf[:, 0:NC], T.gf[:, 0:NC], 32767, None, A.bitwise_and, None, ("gf",), ("jf",))
        weave(rest[1:2], [])
        ts(fo[:], T.jf[:, 0:NC], 8.0, 262144.0, A.mult, A.add, ("jf",), (fn,))
        weave(rest[2:], [])
        tt(T.sp[:], fo[:].indirect(T.rep[:, 0:NC]), T.pw[:], A.mult, (fn, "rep", "pw"), ("sp",))
        cp(T.gp[:, 0:NC], T.pp[:, 0:NC], (), ("gp",), ("pp",))
        ts(T.s12[:], T.sp[:], 15, 4095, A.logical_shift_right, A.bitwise_and, ("sp",), ("s12",))
        ts(T.jp[:, 0:NC], T.gp[:, 0:NC], 32767, None, A.bitwise_and, None, ("gp",), ("jp",))
        ts(T.bit[:], T.sp[:, 0:48], 12, 32768, A.logical_shift_right, A.bitwise_and, ("sp",), ("bit",))
        ts(T.qw[:, 0:NC], T.jp[:, 0:NC], 1.0 / 64, 297.0, A.mult, A.add, ("jp",), ("qw",))
        ts(T.rw[:, 0:NC], T.jp[:, 0:NC], 4904.0 / 128, None, A.mult, None, ("jp",), ("rw0",))
        tt(T.w1[:], T.qw[:, 0:NC].indirect(T.rep[:, 0:NC]), T.s12[:], A.mult, ("qw", "rep", "s12"), ("w1",))
        tt(T.rw[:, 16:64], T.rw[:, 0:NC].indirect(T.rep[:, 0:3]), T.bit[:], A.add, ("rw0", "rep", "bit"), ("rw1",))
        tt(T.w2[:], T.rw[:].indirect(T.rep2[:, 0:NC]), T.w1[:], A.add, ("rw0", "rw1", "rwp", "rep2a", "rep2b", "w1"), ("w2",))
        cp(T.pfb[:], T.jp[:, 0:NC].indirect(T.back[:, 0:1]), ("jp", "back"), ("pfb",))
        ts(T.hw[:, NC:NC + L], T.w2[:], 3, W - 1, A.logical_shift_right, A.bitwise_and, ("w2",), ("hw",))
        cp(T.pf[:, 0:NC], T.jp[:, 0:NC], ("jp",), ("pf",))
        cp(T.hu[:], T.hw[:, NC:NC + L], ("hw",), ("hu",))

    ts(T.ident[:], T.colf[:, 0:128], c(CP), None, A.is_equal, None, ("colf", "cP"), ("ident",))
    ts(c(CP16), c(CP), 16.0, None, A.mult, None, ("cP",), ("cP16",))
    ts(c(CWN), c(CM), -4.0, 1.0, A.mult, A.add, ("cM",), ("cWN",))
    ts(T.pj[:, 3:4], T.pi[:, 0:1], 4, 1, A.logical_shift_right, A.bitwise_and, ("pi",), ("pj3",))
    ts(c(CFU), c(CM), 1.0, -BIG, A.is_equal, A.mult, ("cM",), ("cFU",))
    ts(c(CPP), c(CP), 16.0, None, A.add, None, ("cP",), ("cPP",))
    ts(c(CH0), T.pj[:, 3:4], -float(L), float(L), A.mult, A.add, ("pj3",), ("cH0",))
    ts(c(CH1), T.pj[:, 3:4], float(L), None, A.mult, None, ("pj3",), ("cH1",))
    index(0)
    act(T.identn[:], T.ident[:], F.Copy, ("ident",), ("identn",), scale=-1.0)
    act(T.colb[:], T.s1[:], F.Copy, ("s1",), ("colb",))
    act(T.keep[:], T.c16[:], F.Sign, ("c16",), ("keep",))
    act(T.bfull[:], T.base[:], F.Copy, ("base", "cFU"), ("bfull",), scale=c(CFU))
    act(T.wnew[:], T.onesf[:], F.Copy, ("onesf", "cWN"), ("wnew",), scale=c(CWN))
    act(T.all[:], T.tmp2[:, 0:128], F.Identity, ("tmp2",), ("all",), bias=1.0)
    act(T.spare[:, 0:NC], T.s1[:, 0:NC], F.Identity, ("s1",), ("spare0",), bias=float(W))
    act(T.spare[:, NC:2 * NC], T.s1[:, 0:NC], F.Identity, ("s1",), ("spare1",), bias=float(W))
    ts(T.o8[:], T.blk[0:8, :], T.col[0:8, CP16:CP16 + 1], None, A.is_equal, None, ("blk", "cP16"), ("o8",))
    cp(T.thf[:, 0:1], T.thi[:, 0:1], ("thi",), ("thf",))
    ts(c(CNM), c(CM), -1.0, None, A.mult, None, ("cM",), ("cNM",))
    mm(T.pn[:, 0:1], T.o8[:], T.thf[:, 0:1], True, True, ("o8", "thf"), "pn")
    ts(T.half0[:], T.colf[:, 0:160], c(CPP), c(CH0), A.is_equal, A.mult, ("colf", "cPP", "cH0"), ("half0",))
    ts(T.half1[:], T.colf[:, 0:160], c(CPP), c(CH1), A.is_equal, A.mult, ("colf", "cPP", "cH1"), ("half1",))
    ts(T.thc[:, 0:1], T.pn[:, 0:1], 0.5, None, A.add, None, (), ("thc",), ("pn",))
    ts(T.diag[:], T.c16[:], c(CM), None, A.is_equal, None, ("c16", "cM"), ("diag",))

    def late_constants():
        def first():
            for r4 in range(4):
                fill(T.two[:, SEG[r4]:480:160], 0.0, ("two%d" % r4,) + (("two",) if r4 == 0 else ()))

        def second():
            cp(T.hw[:, 0:NC], T.spare[:, 0:NC], ("spare0",), ("hw0",))
            cp(T.si[:], T.s1[:], ("s1",), ("si",))
            ts(c(CCB), c(CM), -2.0, 1.0, A.mult, A.add, ("cM",), ("cCB",))
            ts(T.sj[:], T.si[:], 63, None, A.bitwise_and, None, ("si",), ("sj",))

        def third():
            ts(c(CTHR), T.s3[:, 0:1], 20.0, None, A.mult, None, ("s3",), ("cTHR",))
            ts(T.ends[:, 0:1], T.s4[:, 3:4], 479.0, None, A.min, None, ("s4d",), ("ends",))
            cp(T.own[:], T.sj[:], ("sj",), ("own",))
        return [first, second, third]

    def small_constants():
        ts(T.pj[:, 1:2], T.pj[:, 0:1], 2, None, A.logical_shift_right, None, ("pj0",), ("pj1",))
        ts(T.pj[:, 2:3], T.pj[:, 0:1], 3, None, A.bitwise_and, None, ("pj0",), ("pj2",))
        tt(T.s2[:], T.pw[:, 0:L:NC], T.diag[:, 0:16], A.mult, ("pw", "diag"), ("s2",))
        ts(T.s4[:, 0:1], T.pj[:, 2:3], 8.0, 8.0, A.mult, A.add, ("pj2",), ("s4a",))
        ts(T.s4[:, 1:2], T.pj[:, 2:3], 2.0, None, A.add, None, ("pj2",), ("s4b",))
        ts(T.s4[:, 2:3], T.pj[:, 1:2], 160.0, -1.0, A.mult, A.add, ("pj1",), ("s4c",))
        op("v", lambda: V.tensor_reduce(T.s3[:, 0:1], T.s2[:], AxisListType.X, A.add), ("s2",), ("s3",))
        ts(T.s4[:, 3:4], T.s4[:, 0:1], T.s4[:, 1:2], T.s4[:, 2:3], A.mult, A.add, ("s4a", "s4b", "s4c"), ("s4d",))

    small_constants()
    cp(T.bf[:, 0:2], T.wprev[:, 0:2], ("wprev",), ("bf",))
    act(T.bb[:], T.base[:], F.Copy, ("base", "bf"), ("bb",), scale=T.bf[:, 1:2])
    TWO = ("two", "two1", "two2", "two3")

    RAW = ["raw%d" % k for k in range(16)]

    def spans(en):
        return tuple(en + str(cc) for cc in range(NC))

    def counters():
        return [lambda ch=ch: cp(T.C[:].indirect(T.nu[:, 4 * ch:4 * ch + 4]), T.nc[:, 64 * ch:64 * ch + 64], ("nu", "nc"), ("C",))
                for ch in (2, 1, 0)]

    bound = [
        lambda: cp(T.mi[:, 0:1], T.pt[:, 0:1], (), ("mi",), ("pt",)),
        lambda: ts(T.mj[:, 0:1], T.mi[:, 0:1], 15, None, A.bitwise_and, None, ("mi",), ("mj",)),
        lambda: ts(T.mcol[:, 0:1], T.mj[:, 0:1], T.thc[:, 0:1], None, A.add, None, ("mj", "thc"), ("mcol",)),
    ]

    for t in range(STEPS):
        z, zn = T["zin%d" % t], "zin%d" % t
        zo, zon = T["zout%d" % t], "zout%d" % t
        last = t == STEPS - 1
        mcol, mname = (T.thc, "thc") if t == 0 else (T.mcol, "mcol")
        if not last:
            send(nxt, T.fin[:, (t + 1) * NC:(t + 2) * NC], T["fout%d" % t][:], "af%d" % (t + 1), "of%d" % t, ("fout%d" % t,))
        mm(T.pz[:, 0:L], T.ident[:], z[:], True, True, ("ident", zn), "pz")
        mm(T.pz[:, L:2 * L], T.ident[:], z[:], True, True, ("ident", zn), "pz")
        mm(T.pd[:, 0:L], T.onesn[:], z[:], True, False, ("onesn", zn), "pd")
        if t == 0:
            dma("g", "lc", T.C[0:128:16, 0:W], T.c0[:], ("X",), ("Ca", "Cb", "Cc", "Cd", "Ce"))
            dma("g", "lc", T.C[1:128:16, 0:W], T.c0[:], (), ("C",))
        mm(T.po[:, 0:NC:2], T.ident[:], T.colb[:, 0:NC:2], True, False, ("ident", "colb"), "po")
        for m in range(16):
            mm(T.pr[:, 15 - m:L:16], T.row[:, 128 * m:128 * m + 128], T.pfb[:, 0:NC], True, True, ("row%d" % m, "pfb"), "pr")
        parts = [[a, a + 1] for a in range(0, OWN - 2, 2)] + [[a] for a in range(OWN - 2 + OWN % 2, OWN)]
        mine = [list(range(a, min(a + 2, 15))) for a in range(OWN, 15, 2)]
        for ks in parts:
            a, b = ks[0], ks[-1] + 1
            act(T.raw[:, a * L:b * L], T.X[:, 0:W].indirect(T.hu[:, a * NC:b * NC]), F.Copy, ("X", "hu"), RAW[a:b])
        cp(T.raw[:, OWN * L:16 * L], T.X[:, 0:W].indirect(T.hu[:, OWN * NC:L]), ("X", "hu"), RAW[OWN:16])
        todo = parts[0:1] + mine + parts[1:]
        for ks in todo:
            a, b = ks[0], ks[-1] + 1
            if t and ks in todo[-3:]:
                bound[todo[-3:].index(ks)]()
            if ks == parts[1]:
                mm(T.pk[:, 0:L], T.ident[:], T.raw[:, 15 * L:16 * L], True, False, ("ident", RAW[15]), "pk")
                mm(T.pk[:, 0:L], T.ident[:], z[:], False, True, ("ident", zn), "pk")
            tt(T.mx[:, a * L:b * L], T.raw[:, a * L:b * L], T.pz[:, 0:(b - a) * L], A.max, RAW[a:b], ["mx%d" % k for k in ks], ("pz",))
            for k in ks:
                mm(T.pd[:, 0:L], T.bn[:, k:128 + k], T.raw[:, k * L:(k + 1) * L], False, False, ("bn", RAW[k]), "pd")
            for k in ks:
                mm(T.pd[:, 0:L], T.b2[:, k:128 + k], T.mx[:, k * L:(k + 1) * L], False, k == todo[-1][-1], ("b2", "mx%d" % k), "pd")
        for cc in range(NC):
            lo, hi = L - 16 * (cc + 1), L - 64 * (cc // 4)
            act(T.er[:, SEG[cc]:SEG[cc] + hi - lo], T.pr[:, lo:hi], F.Abs, ("pf",), ("er%d" % cc,), ("pr",),
                bias=T.pf[:, cc:cc + 1], scale=-1.0)
        act(T.r1[:], T.pk[:, 0:L], F.Identity, (), ("r1",), ("pk",), bias=127.75, scale=0.5)
        act(T.rv[:], T.r1[:], F.Identity, ("r1",), ("rv",), bias=-128.0)
        roots = [
            lambda: scan(T.sr[:], T.one[:], T.er[:], 0.0, A.add, A.min, ("one",) + spans("er"), ("sr",)),
            lambda: tt(T.lr[:], T.sr[:].indirect(T.ends[:, 0:1]), T.own[:], A.is_lt, ("sr", "ends", "own"), ("lr",)),
            lambda: tt(T.ar[:, 0:NC], T.lr[:, 0:NC], T.spare[:, 0:NC], A.mult, ("lr", "spare0"), ("ar",)),
            lambda: tt(T.ar2[:, 0:NC], T.ar[:, 0:NC], T.hw[:, L:NC + L], A.max, ("ar", "hw"), ("ar2",)),
            lambda: cp(T.ru[:, 0:NC], T.ar2[:, 0:NC], ("ar2",), ("ru",)),
        ]
        gaps = counters() if t else late_constants()
        gaps[0]()
        ts(T.miss[:], T.pd[:, 0:L], mcol[:, 0:1], None, A.is_gt, None, (mname,), ("miss",), ("pd",))
        op("v", lambda: V.transpose(T.turned[:], T.miss[:]), ("miss",), ("turned",))
        scan(T.js[:], T.turned[:], T.turned[:], 0.0, A.mult, A.add, ("turned",), ("js",))
        mm(T.po[:, 0:NC:2], T.half0[:, 16:144], T.js[:, 15:L:32], False, False, ("half0", "js"), "po")
        mm(T.po[:, 0:NC:2], T.half0[:, 0:128], T.js[:, 31:L:32], False, True, ("half0", "js"), "po")
        mm(T.po[:, 1:NC:2], T.ident[:], T.colb[:, 1:NC:2], True, False, ("ident", "colb"), "po")
        mm(T.po[:, 1:NC:2], T.half1[:, 32:160], T.js[:, 15:L:32], False, False, ("half1", "js"), "po")
        mm(T.po[:, 1:NC:2], T.half1[:, 16:144], T.js[:, 31:L:32], False, True, ("half1", "js"), "po")
        if not last:
            act(T.top[:, 0:NC], T.js[:, 15:L:16], F.Relu, ("js",), ("top", "acc"), bias=-14.0, accum_out=T.acc[:, 0:1])
        gaps[1]()
        cp(T.offu[:, 0:NC], T.po[:, 0:NC], (), ("offu",), ("po",))
        ts(T.off2[:, 0:NC], T.po[:, 0:NC], c(CNM), 1.0 / 16, A.add, A.mult, ("cNM",), ("off2",), ("po",))
        dzs = DZS or last
        if dzs:
            act(T.yv[:], T.raw[:].indirect(T.offu[:, 0:NC]), F.Copy, RAW + ["offu"], ("yv",))
            mm(T.pp[:, 0:L], T.identn[:], z[:], True, False, ("identn", zn), "pp")
            mm(T.pp[:, 0:L], T.ident[:], T.yv[:], False, True, ("ident", "yv"), "pp")
            act(zo[:], T.pp[:, 0:L], F.Abs, (), (zon,), ("pp",))
        else:
            tt(T.dz[:], T.raw[:].indirect(T.offu[:, 0:NC]), z[:], A.subtract, RAW + ["offu", zn], ("dz",))
            act(zo[:], T.dz[:], F.Abs, ("dz",), (zon,))
        if not last:
            send(nxt, T["zin%d" % (t + 1)][:], zo[:], "az%d" % (t + 1), "oz%d" % t, (zon,))
        if t:
            send(rank - HOP * t, T.home[:, t * L:(t + 1) * L], zo[:], "ah%d" % t, "oh%d" % t, (zon,))
            dma("y", "st%d" % t, T.zs[:, t * L:(t + 1) * L], T.home[:, t * L:(t + 1) * L], ("home%d" % t,), ())
        else:
            dma("y", "st0", T.zs[:, 0:L], zo[:], (zon,), ())
        tt(T.gm[:], T.hw[:, 0:NC + L].indirect(T.off2[:, 0:NC]), T.diag[:], A.mult, ("hw", "hw0", "off2", "diag"), ("gm",))
        mm(T.pk[:, 0:L], T.onesf[:], T.gm[:], True, True, ("onesf", "gm"), "pk")
        if not last:
            mm(T.pt[:, 0:1], T.all[:], T.acc[:, 0:1], True, True, ("all", "acc"), "pt")
        gaps[2]()
        scan(T.ks[:], T.keep[:], T.gm[:], 0.0, A.mult, A.add, ("keep", "gm"), ("ks",))
        cp(T.keyu[:, 0:NC], T.ks[:, 15:L:16], ("ks",), ("keyu",))
        if not dzs:
            act(T.yv[:], T.raw[:].indirect(T.offu[:, 0:NC]), F.Copy, RAW + ["offu"], ("yv",))
        act(T.cr[:], T.C[:].indirect(T.keyu[:, 0:NC]), F.Relu, ("C", "keyu", "cCB"), ("cr",), bias=c(CCB))
        mm(T.po[:, 0:NC], T.ident[:], T.bigb[:, 0:NC], True, False, ("ident", "bigb"), "po")
        packed(T.po[:, 0:NC], T.bfull, "bfull", T.cr, "cr", False, "po")
        mm(T.pz[:, 0:L], T.wnew[:], T.cr[:], True, True, ("wnew", "cr"), "pz")
        act(T.nc[:], T.pz[:, 0:L], F.Copy, (), ("nc",), ("pz",))
        for cc in range(NC):
            lo, hi = 64 * (cc // 4), 16 * (cc + 1)
            ts(T.en[:, SEG[cc]:SEG[cc] + hi - lo], T.pk[:, lo:hi], T.ks[:, 16 * cc + 15:16 * cc + 16], None, A.is_equal, None,
               ("ks",), ("en%d" % cc,), ("pk",))
        scan(T.sn[:], T.two[:], T.en[:], 0.0, A.mult, A.add, TWO + spans("en"), ("sn",))
        weave(roots[:2], [
            lambda: ts(T.ln[:], T.sn[:].indirect(T.ends[:, 0:1]), c(CTHR), BIG, A.is_gt, A.mult, ("sn", "ends", "cTHR"), ("ln",)),
            lambda: tt(T.an[:, 0:NC], T.ln[:, 0:NC], T.ks[:, 15:L:16], A.add, ("ln", "ks"), ("an0",)),
            lambda: tt(T.an[:, NC:24], T.po[:, 0:NC], T.an[:, 0:NC], A.add, ("an0",), ("an1",), ("po",)),
            lambda: tt(T.an2[:, 0:24], T.an[:, 0:24], T.spare[:, 0:24], A.min, ("an0", "an1", "spare0", "spare1"), ("an2",)),
            lambda: cp(T.nu[:, 0:24], T.an2[:, 0:24], ("an2",), ("nu",)),
        ])
        for ch in (2, 1, 0):
            roots[4 - ch]()
            cp(T.X[:].indirect(T.nu[:, NC + 4 * ch:NC + 4 * ch + 4]), T.yv[:, 64 * ch:64 * ch + 64], ("nu", "yv"), ("X",))
        tops = [lambda ch=ch: cp(T.X[:].indirect(T.ru[:, 4 * ch:4 * ch + 4]), T.rv[:, 64 * ch:64 * ch + 64], ("ru", "rv"), ("X",))
                for ch in (2, 1, 0)]
        if last:
            weave(tops, [])
        else:
            weave(tops[:3 - LATE], [])
            index(t + 1, tops[3 - LATE:])

    for f in counters():
        f()
    dma("g", "oc", T.cs[:], T.C[0:128:16, 0:W], ("C",), ())
    n, span = 512 // PIECES, W // PIECES
    for h, pb in enumerate(("pk", "pr", "pp", "pn")[:PIECES]):
        xo = "xo%d" % h
        for q in range(16):
            a = h * span + n * q
            mm(T[pb][:, 0:n], T.ba[:, 15 - q:143 - q], T.X[:, a:a + n], q == 0, q == 15, ("ba", "X"), pb)
        act(T.xo[:, h * n:(h + 1) * n], T[pb][:, 0:n], F.Copy, (), (xo,), (pb,), scale=1.0 / 128)
        dma("y", "ox%d" % h, T.xs[:, h * span:(h + 1) * span], T.xo[:, h * n:(h + 1) * n], (xo,), ())
    for name in sorted(total, key=lambda k: (k[:2] == "ox", k == "oc", k)):
        wait("g", (name, total[name]))
